import numpy as np
import ml_dtypes


def mxq(x, axis, fmt="e4m3"):
    dtype, down = {"e4m3": (ml_dtypes.float8_e4m3fn, 7), "e5m2": (ml_dtypes.float8_e5m2, 14)}[fmt]
    v = np.moveaxis(np.asarray(x, np.float32).astype(ml_dtypes.bfloat16).astype(np.float64), axis, -1)
    blocks = v.reshape(v.shape[:-1] + (-1, 32))
    amax = np.abs(blocks).max(-1, keepdims=True)
    byte = np.maximum(np.where(amax > 0, np.frexp(amax)[1] - 1 + 127, 0) - down, 1)
    scale = np.exp2(byte - 127.0)
    codes = (blocks / scale).astype(np.float32).astype(dtype).astype(np.float64)
    return np.moveaxis((codes * scale).reshape(v.shape), -1, axis)


WIDE = False


def mx_kscale(k):
    if not WIDE:
        return np.ones(k)
    levels = np.array([10, -10, 5, -5, 0])
    if k % 512:
        return np.exp2(np.random.permutation(np.resize(levels, k // 32))).repeat(32)
    a = np.empty((k // 512, 16))
    for p in range(k // 512):
        a[p, :8] = np.random.permutation(np.resize(levels, 8))
        for g in range(8):
            far = levels[np.abs(levels - a[p, g]) >= 10]
            a[p, g + 8] = far[np.random.randint(len(far))]
    return np.exp2(a.ravel()).repeat(32)


def f64(x):
    return np.asarray(x).astype(np.float64)


def striped(idx):
    return np.tile(np.asarray(idx).reshape(-1, 16).T, (8, 1)).astype(np.uint16)


def unstriped(offs):
    return offs[:16].T.reshape(-1).astype(np.int64)


E2M1 = np.array([0.0, 0.5, 1.0, 1.5, 2.0, 3.0, 4.0, 6.0, -0.0, -0.5, -1.0, -1.5, -2.0, -3.0, -4.0, -6.0])


def pack_weight(w, fmt):
    k, n = w.shape
    w = f64(np.asarray(w, np.float32).astype(ml_dtypes.bfloat16)).reshape(k // 32, 32, n)
    amax = np.abs(w).max(1)
    if fmt == "e4m3":
        byte = np.frexp(amax)[1] - 1 + 127 - 7
    else:
        mant, ex = np.frexp(amax / 6.0)
        byte = np.where(mant > 0.5, ex, ex - 1) + 127
    byte = np.clip(np.where(amax > 0, byte, 1), 1, 254)
    scaled = (w * np.exp2(127.0 - byte)[:, None, :]).reshape(k, n).astype(np.float32)
    by_word = np.ascontiguousarray(scaled.reshape(k // 512, 128, 4, n).transpose(0, 1, 3, 2))
    if fmt == "e4m3":
        words = by_word.astype(ml_dtypes.float8_e4m3fn).view(np.uint8)
    else:
        c = by_word.astype(ml_dtypes.float4_e2m1fn).view(np.uint8) & 0xF
        words = (c[..., 0::2] | (c[..., 1::2] << 4)).reshape(k // 512, 128, 2 * n)
    return np.ascontiguousarray(words), np.ascontiguousarray(byte.astype(np.uint8).reshape(k // 512, 16, n))


def unpack_weight(words, scales, fmt):
    g, _, n = scales.shape
    words = np.ascontiguousarray(words).reshape(g, 128, n, -1)
    if fmt == "e4m3":
        vals = words.view(ml_dtypes.float8_e4m3fn).astype(np.float64)
    else:
        nib = np.empty((g, 128, n, 4), np.uint8)
        nib[..., 0::2] = words & 0xF
        nib[..., 1::2] = words >> 4
        vals = E2M1[nib]
    vals = vals * np.repeat(np.exp2(scales.astype(np.float64) - 127.0), 8, axis=1)[..., None]
    return vals.transpose(0, 1, 3, 2).reshape(g * 512, n)


def sigmoid(v):
    return 1.0 / (1.0 + np.exp(-v))


D, T, U, I, J = 512, 1024, 1024, 256, 512


def setup_inputs():
    n = np.random.standard_normal
    idx3 = np.random.permutation(J)[:J]
    idx = np.random.permutation(T)[:I]
    idx2 = np.random.permutation(U)[:J]
    fd = mx_kscale(D)
    fj = mx_kscale(J)
    tj = np.ones(U)
    tj[idx2] = fj
    tabbp = pack_weight(n((D, U)) / fd[:, None], "e2m1")
    return {
        "taba": (n((D, T)) * 1 / np.sqrt(D) * fd[:, None]).astype(np.float32),
        "tabb_words": tabbp[0],
        "tabb_scales": tabbp[1],
        "pw": (np.random.uniform(-1.5, 1.5, (1, J))).astype(np.float32),
        "js": (np.random.uniform(0.5, 2.0, (1, J)) * fj).astype(np.float32),
        "brows": (n((D, U)) / tj).astype(np.float32),
        "old": (n((D, T)) * 2.0).astype(np.float32),
        "fade": (np.random.uniform(0.5, 1.0, (1, T))).astype(np.float32),
        "offs3": striped(idx3),
        "offs": striped(idx),
        "offs2": striped(idx2),
    }


def reference(taba, tabb_words, tabb_scales, pw, js, brows, old, fade, offs3, offs, offs2):
    idx3 = unstriped(offs3)
    idx = unstriped(offs)
    idx2 = unstriped(offs2)
    tabbu = unpack_weight(tabb_words, tabb_scales, "e2m1")
    tabaidxq = mxq(f64(taba)[:, idx], 0, "e4m3")
    tabbidx2g = tabbu[:, idx2]
    s = tabaidxq.T @ tabbidx2g
    g1 = sigmoid(s)
    e1 = f64(pw) * s
    s1 = np.zeros((I, J))
    s1[:, idx3] = e1
    ds = f64(pw) * g1[:, idx3] + s1 * g1 * (1.0 - g1)
    gs = ds * f64(js)
    gt1 = gs.T
    bt = f64(brows)[:, idx2].T
    btq = mxq(bt, 0, "e4m3")
    gt1q = mxq(gt1, 0, "e4m3")
    gx1 = btq.T @ gt1q
    gf = np.zeros((D, T))
    gf[:, idx] = gx1
    y = f64(old) * f64(fade) + gf
    return y

@@ -1,0 +1,267 @@
+from contextlib import ExitStack
+
+import concourse.mybir as mybir
+from concourse.masks import make_identity
+
+D, T, U, I, J = 512, 1024, 1024, 256, 512
+FLOPS = 2 * D * I * J * 2
+
+F32 = mybir.dt.float32
+BF16 = mybir.dt.bfloat16
+I32 = mybir.dt.int32
+U32 = mybir.dt.uint32
+U16 = mybir.dt.uint16
+U8 = mybir.dt.uint8
+FP8X4 = mybir.dt.float8_e4m3fn_x4
+FP4X4 = mybir.dt.float4_e2m1fn_x4
+ACT = mybir.ActivationFunctionType
+ALU = mybir.AluOpType
+
+P = 128
+PACK = 4
+BANK = 512
+S1_WINDOW = 704
+
+
+def tile_attend_bpairlink_x_kernel(tc, taba, tabb_words, tabb_scales, pw, js, brows, old, fade, offs3, offs, offs2, out):
+    nc = tc.nc
+    with ExitStack() as ctx:
+        lists = ctx.enter_context(tc.tile_pool(name="lists", bufs=1))
+        sb = ctx.enter_context(tc.tile_pool(name="sb", bufs=1))
+        psum = ctx.enter_context(tc.psum_pool(name="psum", bufs=1))
+
+        def bank(n, name):
+            return psum.tile([P, BANK], F32, name=name, tag="bank%d" % n)
+
+        def quarters(ap):
+            return ap.rearrange("p (t c) -> p t c", t=PACK)
+
+        o2 = lists.tile([P, J // 16], U16, name="o2")
+        o1 = lists.tile([P, I // 16], U16, name="o1")
+        o3 = lists.tile([P, J // 16], U16, name="o3")
+
+        zero = sb.tile([P, 1], F32, name="zero")
+        nc.gpsimd.memset(zero[:], 0.0)
+        sc_win = sb.tile([P, U], U8, name="sc_win", tag="a_in", align_bytes=64)
+        nc.gpsimd.memset(sc_win[:].bitcast(I32), 0)
+        pw_col = sb.tile([P, PACK], F32, name="pw_col")
+        nc.scalar.dma_start(pw_col[:], pw.rearrange("o (p t) -> (o p) t", t=PACK))
+        half = sb.tile([P, 1], F32, name="half")
+        nc.scalar.activation(half[:], zero[:], ACT.Sigmoid)
+
+        nc.sync.dma_start(o2[:], offs2)
+        w_win = sb.tile([P, U], U16, name="w_win", tag="b_raw0")
+        nc.sync.dma_start(w_win[:].bitcast(I32), tabb_words[0].bitcast(I32))
+        for q in range(4):
+            nc.scalar.dma_start(sc_win[32 * q : 32 * q + 4, :].bitcast(I32), tabb_scales[0, 4 * q : 4 * q + 4, :].bitcast(I32))
+        nc.sync.dma_start(o1[:], offs)
+        a_rows = taba.rearrange("(p t) c -> p t c", t=PACK)
+        a01 = sb.tile([P, 2, T], F32, name="a01", tag="b_raw1")
+        nc.sync.dma_start(a01[:], a_rows[:, 0:2, :])
+        a2 = sb.tile([P, T], F32, name="a2", tag="old0")
+        nc.sync.dma_start(a2[:], a_rows[:, 2, :])
+        a3 = sb.tile([P, T], F32, name="a3", tag="old1")
+        nc.sync.dma_start(a3[:], a_rows[:, 3, :])
+        nc.sync.dma_start(o3[:], offs3)
+
+        ident = sb.tile([P, P], F32, name="ident")
+        make_identity(nc, ident[:])
+
+        js_col = sb.tile([P, PACK], F32, name="js_col")
+        nc.gpsimd.dma_start(js_col[:], js.rearrange("o (p t) -> (o p) t", t=PACK))
+        fade_rows = sb.tile([P, P], F32, name="fade_rows")
+        nc.gpsimd.memset(fade_rows[:], 0.0)
+        nc.gpsimd.dma_start(fade_rows[0 : T // P, :], fade.rearrange("o (c p) -> (o c) p", p=P))
+
+        gf = []
+        for k in range(4):
+            t = sb.tile([P, T], F32, name="gf%d" % k)
+            nc.vector.memset(t[:], 0.0)
+            gf.append(t)
+
+        pw_ps = bank(2, "pw_ps")
+        for t in range(PACK):
+            nc.tensor.transpose(pw_ps[:, P * t : P * (t + 1)], pw_col[:, t : t + 1].to_broadcast([P, P]), ident[:])
+        pw_b = sb.tile([P, J], F32, name="pw_b")
+        npw_b = sb.tile([P, J], F32, name="npw_b")
+        pw_nat = quarters(pw_ps[:]).rearrange("p t c -> p c t")
+        nc.scalar.activation(npw_b[:].rearrange("p (c t) -> p c t", t=PACK), pw_nat, ACT.Copy, scale=-1.0)
+        nc.scalar.activation(pw_b[:].rearrange("p (c t) -> p c t", t=PACK), pw_nat, ACT.Copy)
+        njs = sb.tile([P, PACK], F32, name="njs")
+        nc.scalar.activation(njs[:], js_col[:], ACT.Copy, scale=-1.0)
+        fade_ps = bank(3, "fade_ps")
+        nc.tensor.transpose(fade_ps[:, 0:P], fade_rows[:], ident[:])
+        fade_col = sb.tile([P, T // P], F32, name="fade_col")
+        nc.scalar.copy(fade_col[:], fade_ps[:, 0 : T // P])
+
+        w_g = sb.tile([P, J], U16, name="w_g", align_bytes=64)
+        nc.vector.tensor_copy(w_g[:], w_win[:].indirect(o2[:]))
+        sc_g = sb.tile([P, J], U8, name="sc_g", align_bytes=64)
+        nc.vector.tensor_copy(sc_g[:], sc_win[:].indirect(o2[:]))
+
+        a_pair = sb.tile([P, T], U32, name="a_pair")
+        a_pair_values = a_pair[:].bitcast(BF16).rearrange("p (c e) -> p c e", e=2)
+        nc.scalar.activation(a_pair_values, a01[:].rearrange("p e c -> p c e"), ACT.Copy)
+        a_in = sb.tile([P, I, PACK], BF16, name="a_in", tag="a_in", align_bytes=64)
+        a_words = a_in[:].rearrange("p c t -> p (c t)").bitcast(U32).rearrange("p (c e) -> p c e", e=2)
+        s_ps = []
+        for n in range(2):
+            cols = slice(P * n, P * (n + 1))
+            lst = o1[:, 8 * n : 8 * n + 8]
+            nc.vector.tensor_copy(a_in[:, cols, 2], a2[:].indirect(lst))
+            nc.vector.tensor_copy(a_words[:, cols, 0], a_pair[:].indirect(lst))
+            nc.vector.tensor_copy(a_in[:, cols, 3], a3[:].indirect(lst))
+            aq = sb.tile([P, P], U32, name="aq%d" % n, tag="aq%d" % n, align_bytes=64)
+            asc = sb.tile([P, P], U8, name="asc%d" % n, align_bytes=64)
+            nc.vector.quantize_mx(out=aq[:].bitcast(FP8X4), scales=asc[:], in_=a_in[:, cols, :].rearrange("p c t -> p (c t)"))
+            ps = bank(n, "s_ps%d" % n)
+            nc.tensor.matmul_mx(out=ps[:], lhsT=aq[:].bitcast(FP8X4), lhsT_scale=asc[:], rhs=w_g[:].bitcast(FP4X4), rhs_scale=sc_g[:], start=True, stop=True)
+            s_ps.append(ps)
+
+        b_raw = []
+        for h in range(2):
+            t = sb.tile([P, 2, U], F32, name="b_raw%d" % h, tag="b_raw%d" % h)
+            nc.sync.dma_start(t[:], brows[256 * h : 256 * (h + 1), :].rearrange("(p e) u -> p e u", e=2))
+            b_raw.append(t)
+
+        old_rows = old.rearrange("(k p) t -> p k t", p=P)
+        old_sb = []
+        for h in range(2):
+            t = sb.tile([P, 2, T], F32, name="old%d" % h, tag="old%d" % h)
+            nc.sync.dma_start(t[:], old_rows[:, 2 * h : 2 * h + 2, :])
+            old_sb.extend([t[:, 0, :], t[:, 1, :]])
+
+        g = [sb.tile([P, J], F32, name="g%d" % n) for n in range(2)]
+        s = [sb.tile([P, J], F32, name="s%d" % n) for n in range(2)]
+        sq = [sb.tile([P, J], F32, name="sq%d" % n) for n in range(2)]
+        halves = [(slice(256 * u, 256 * (u + 1)), o3[:, 16 * u : 16 * (u + 1)]) for u in range(2)]
+
+        def sigmoid(n):
+            nc.scalar.activation(g[n][:], s_ps[n][:], ACT.Sigmoid)
+
+        def scores_out(n):
+            nc.scalar.copy(s[n][:], s_ps[n][:])
+
+        def square(n):
+            nc.scalar.activation(sq[n][:], g[n][:], ACT.Square, bias=half[:], scale=-1.0)
+
+        def linked(n, tag):
+            a_term = sb.tile([P, J], F32, name="a_term%d" % n, tag=tag, align_bytes=64)
+            for cols, lst in halves:
+                nc.vector.tensor_tensor(a_term[:, cols], g[n][:].indirect(lst), npw_b[:, cols], ALU.mult)
+            return a_term
+
+        def placed(n, tag):
+            s1 = sb.tile([P, S1_WINDOW], F32, name="s1_%d" % n, tag=tag, align_bytes=64)
+            nc.vector.tensor_tensor(s1[:].indirect(o3[:]), s[n][:], pw_b[:], ALU.mult)
+            return s1
+
+        def slope_term(n, s1, tag):
+            b_term = sb.tile([P, J], F32, name="b_term%d" % n, tag=tag, align_bytes=64)
+            nc.vector.scalar_tensor_tensor(b_term[:], sq[n][:], 0.25, s1[:, 0:J], ALU.subtract, ALU.mult)
+            return b_term
+
+        def turn(n, a_term, b_term, where):
+            ps = bank(where, "gs_ps%d" % n)
+            for m, term in enumerate((a_term, b_term)):
+                for t in range(PACK):
+                    nc.tensor.matmul(ps[:, P * t : P * (t + 1)], lhsT=term[:, t : J : PACK], rhs=ident[:], is_transpose=True,
+                                     start=(m == 0 and t == 0), stop=(m == 1 and t == PACK - 1))
+            return ps
+
+        gq = sb.tile([P, I], U32, name="gq", align_bytes=64)
+        gsc = sb.tile([P, I], U8, name="gsc", align_bytes=64)
+
+        def scale_round(n, ps, g_both):
+            g_in = g_both[:, P * n : P * (n + 1), :]
+            nc.vector.tensor_tensor(g_in, quarters(ps[:]).rearrange("p t c -> p c t"), njs[:].unsqueeze(1).to_broadcast([P, P, PACK]), ALU.mult)
+            cols = slice(P * n, P * (n + 1))
+            nc.vector.quantize_mx(out=gq[:, cols].bitcast(FP8X4), scales=gsc[:, cols], in_=g_in.rearrange("p c t -> p (c t)"))
+
+        def quantise(name, src, width):
+            q = sb.tile([P, width], U32, name=name + "q", align_bytes=64)
+            sc = sb.tile([P, width], U8, name=name + "s", align_bytes=64)
+            nc.vector.quantize_mx(out=q[:].bitcast(FP8X4), scales=sc[:], in_=src[:].rearrange("p c t -> p (c t)"))
+            return q, sc
+
+        def cast_pair(h, tag):
+            pair = sb.tile([P, U], F32, name="pair%d" % h, tag=tag, align_bytes=64)
+            values = pair[:].bitcast(BF16).rearrange("p (u e) -> p u e", e=2)
+            for u in range(2):
+                cols = slice(512 * u, 512 * (u + 1))
+                nc.scalar.activation(values[:, cols, :], b_raw[h][:, :, cols].rearrange("p e u -> p u e"), ACT.Copy)
+            return pair
+
+        def gather_words(h, pair):
+            words = sb.tile([P, J], F32, name="bw%d" % h)
+            nc.vector.tensor_copy(words[:], pair[:].indirect(o2[:]))
+            return words
+
+        def turn_words(h, words, where):
+            ps = bank(where, "bt_ps%d" % h)
+            for t in range(PACK):
+                nc.tensor.transpose(ps[:, P * t : P * (t + 1)], words[:, t : J : PACK], ident[:])
+            b_in = sb.tile([P, 2 * P, PACK], BF16, name="b_in%d" % h, tag="b_in%d" % h, align_bytes=64)
+            nc.scalar.copy(b_in[:], quarters(ps[:].bitcast(BF16)).rearrange("p t c -> p c t"))
+            return b_in
+
+        def product(h, bq, where):
+            ps = bank(where, "gx_ps%d" % h)
+            q, sc = bq
+            gx = []
+            for e in range(2):
+                cols = slice(P * e, P * (e + 1))
+                nc.tensor.matmul_mx(out=ps[:, I * e : I * (e + 1)], lhsT=q[:, cols].bitcast(FP8X4), lhsT_scale=sc[:, cols],
+                                    rhs=gq[:].bitcast(FP8X4), rhs_scale=gsc[:], start=True, stop=True)
+            for e in range(2):
+                part = sb.tile([P, I], F32, name="gx%d_%d" % (h, e))
+                nc.scalar.copy(part[:], ps[:, I * e : I * (e + 1)])
+                gx.append(part)
+            return gx
+
+        def finish(k, gx, banks, tags):
+            nc.vector.tensor_copy(gf[k][:].indirect(o1[:]), gx[:])
+            for u in range(2):
+                ps = bank(banks[u], "back%d_%d" % (k, u))
+                for c in range(4):
+                    nc.tensor.transpose(ps[:, P * c : P * (c + 1)], faded[4 * u + c][:, P * k : P * (k + 1)], ident[:])
+                res = sb.tile([P, BANK], F32, name="res%d_%d" % (k, u), tag=tags[u], align_bytes=64)
+                cols = slice(BANK * u, BANK * (u + 1))
+                nc.vector.tensor_tensor(res[:], ps[:], gf[k][:, cols], ALU.add)
+                nc.sync.dma_start(out[P * k : P * (k + 1), cols], res[:])
+
+        sigmoid(0)
+        scores_out(0)
+        square(0)
+        pair0 = cast_pair(0, "aq1")
+        sigmoid(1)
+        pair1 = cast_pair(1, "pair1")
+        scores_out(1)
+        square(1)
+
+        a0 = linked(0, "a_term0")
+        b0 = slope_term(0, placed(0, "s1_0"), "b_term0")
+        gs0 = turn(0, a0, b0, 2)
+        b_in0 = turn_words(0, gather_words(0, pair0), 4)
+        a1 = linked(1, "aq1")
+        b_in1 = turn_words(1, gather_words(1, pair1), 5)
+        bq0 = quantise("b0", b_in0, 2 * P)
+        b1 = slope_term(1, placed(1, "pair1"), "b_term1")
+        gs1 = turn(1, a1, b1, 3)
+        g_both = sb.tile([P, I, PACK], BF16, name="g_both", tag="pair1", align_bytes=64)
+        scale_round(0, gs0, g_both)
+        bq1 = quantise("b1", b_in1, 2 * P)
+        scale_round(1, gs1, g_both)
+        gx = product(0, bq0, 4) + product(1, bq1, 5)
+
+        faded = []
+        for c in range(T // P):
+            ps = bank((6, 7, 0, 1)[c % 4], "old_ps%d" % c)
+            for k in range(4):
+                nc.tensor.transpose(ps[:, P * k : P * (k + 1)], old_sb[k][:, P * c : P * (c + 1)], ident[:])
+            f = sb.tile([P, D], F32, name="faded%d" % c)
+            nc.scalar.activation(f[:], ps[:], ACT.Copy, scale=fade_col[:, c : c + 1])
+            faded.append(f)
+
+        for k in range(4):
+            finish(k, gx[k], ((6, 7), (0, 1), (2, 3), (4, 5))[k], ("res%d_0" % k, "res%d_1" % k))

@@ -40,38 +40,32 @@ def tile_attend_bpairlink_x_kernel(tc, taba, tabb_words, tabb_scales, pw, js, br
         o1 = lists.tile([P, I // 16], U16, name="o1")
         o3 = lists.tile([P, J // 16], U16, name="o3")
 
-        zero = sb.tile([P, 1], F32, name="zero")
-        nc.gpsimd.memset(zero[:], 0.0)
+        zero = sb.tile([P, 1], F32, name="zero", tag="old0")
+        nc.vector.memset(zero[:], 0.0)
         sc_win = sb.tile([P, U], U8, name="sc_win", tag="a_in", align_bytes=64)
-        nc.gpsimd.memset(sc_win[:].bitcast(I32), 0)
-        pw_col = sb.tile([P, PACK], F32, name="pw_col")
+        nc.vector.memset(sc_win[:].bitcast(I32), 0)
+        pw_col = sb.tile([P, PACK], F32, name="pw_col", tag="b_raw0")
         nc.scalar.dma_start(pw_col[:], pw.rearrange("o (p t) -> (o p) t", t=PACK))
         half = sb.tile([P, 1], F32, name="half")
         nc.scalar.activation(half[:], zero[:], ACT.Sigmoid)
 
         nc.sync.dma_start(o2[:], offs2)
-        w_win = sb.tile([P, U], U16, name="w_win", tag="b_raw0")
+        w_win = sb.tile([P, U], U16, name="w_win", tag="small")
         nc.sync.dma_start(w_win[:].bitcast(I32), tabb_words[0].bitcast(I32))
-        for q in range(4):
-            nc.scalar.dma_start(sc_win[32 * q : 32 * q + 4, :].bitcast(I32), tabb_scales[0, 4 * q : 4 * q + 4, :].bitcast(I32))
         nc.sync.dma_start(o1[:], offs)
         a_rows = taba.rearrange("(p t) c -> p t c", t=PACK)
         a01 = sb.tile([P, 2, T], F32, name="a01", tag="b_raw1")
         nc.sync.dma_start(a01[:], a_rows[:, 0:2, :])
-        a2 = sb.tile([P, T], F32, name="a2", tag="old0")
-        nc.sync.dma_start(a2[:], a_rows[:, 2, :])
-        a3 = sb.tile([P, T], F32, name="a3", tag="old1")
-        nc.sync.dma_start(a3[:], a_rows[:, 3, :])
+        for q in range(4):
+            nc.sync.dma_start(sc_win[32 * q : 32 * q + 4, :].bitcast(I32), tabb_scales[0, 4 * q : 4 * q + 4, :].bitcast(I32))
         nc.sync.dma_start(o3[:], offs3)
+        a23 = sb.tile([P, 2, T], F32, name="a23", tag="old0")
+        a2, a3 = a23[:, 0, :], a23[:, 1, :]
+        nc.sync.dma_start(a2, a_rows[:, 2, :])
+        nc.sync.dma_start(a3, a_rows[:, 3, :])
 
         ident = sb.tile([P, P], F32, name="ident")
         make_identity(nc, ident[:])
-
-        js_col = sb.tile([P, PACK], F32, name="js_col")
-        nc.gpsimd.dma_start(js_col[:], js.rearrange("o (p t) -> (o p) t", t=PACK))
-        fade_rows = sb.tile([P, P], F32, name="fade_rows")
-        nc.gpsimd.memset(fade_rows[:], 0.0)
-        nc.gpsimd.dma_start(fade_rows[0 : T // P, :], fade.rearrange("o (c p) -> (o c) p", p=P))
 
         gf = []
         for k in range(4):
@@ -87,36 +81,42 @@ def tile_attend_bpairlink_x_kernel(tc, taba, tabb_words, tabb_scales, pw, js, br
         pw_nat = quarters(pw_ps[:]).rearrange("p t c -> p c t")
         nc.scalar.activation(npw_b[:].rearrange("p (c t) -> p c t", t=PACK), pw_nat, ACT.Copy, scale=-1.0)
         nc.scalar.activation(pw_b[:].rearrange("p (c t) -> p c t", t=PACK), pw_nat, ACT.Copy)
-        njs = sb.tile([P, PACK], F32, name="njs")
-        nc.scalar.activation(njs[:], js_col[:], ACT.Copy, scale=-1.0)
-        fade_ps = bank(3, "fade_ps")
-        nc.tensor.transpose(fade_ps[:, 0:P], fade_rows[:], ident[:])
-        fade_col = sb.tile([P, T // P], F32, name="fade_col")
-        nc.scalar.copy(fade_col[:], fade_ps[:, 0 : T // P])
 
         w_g = sb.tile([P, J], U16, name="w_g", align_bytes=64)
         nc.vector.tensor_copy(w_g[:], w_win[:].indirect(o2[:]))
         sc_g = sb.tile([P, J], U8, name="sc_g", align_bytes=64)
         nc.vector.tensor_copy(sc_g[:], sc_win[:].indirect(o2[:]))
 
-        a_pair = sb.tile([P, T], U32, name="a_pair")
+        small = sb.tile([P, P + 8], F32, name="small", tag="small")
+        nc.vector.memset(small[:], 0.0)
+        fade_rows = small[:, 0:P]
+        js_col = small[:, P : P + PACK]
+        nc.sync.dma_start(small[0 : T // P, 0:P], fade.rearrange("o (c p) -> (o c) p", p=P))
+        nc.sync.dma_start(js_col, js.rearrange("o (p t) -> (o p) t", t=PACK))
+        a_pair = sb.tile([P, T], U32, name="a_pair", tag="old1")
         a_pair_values = a_pair[:].bitcast(BF16).rearrange("p (c e) -> p c e", e=2)
         nc.scalar.activation(a_pair_values, a01[:].rearrange("p e c -> p c e"), ACT.Copy)
-        a_in = sb.tile([P, I, PACK], BF16, name="a_in", tag="a_in", align_bytes=64)
-        a_words = a_in[:].rearrange("p c t -> p (c t)").bitcast(U32).rearrange("p (c e) -> p c e", e=2)
         s_ps = []
         for n in range(2):
-            cols = slice(P * n, P * (n + 1))
+            a_in = sb.tile([P, P, PACK], BF16, name="a_in%d" % n, tag="a_in", align_bytes=64)
+            a_words = a_in[:].rearrange("p c t -> p (c t)").bitcast(U32).rearrange("p (c e) -> p c e", e=2)
             lst = o1[:, 8 * n : 8 * n + 8]
-            nc.vector.tensor_copy(a_in[:, cols, 2], a2[:].indirect(lst))
-            nc.vector.tensor_copy(a_words[:, cols, 0], a_pair[:].indirect(lst))
-            nc.vector.tensor_copy(a_in[:, cols, 3], a3[:].indirect(lst))
+            nc.vector.tensor_copy(a_in[:, :, 2], a2.indirect(lst))
+            nc.vector.tensor_copy(a_in[:, :, 3], a3.indirect(lst))
+            nc.vector.tensor_copy(a_words[:, :, 0], a_pair[:].indirect(lst))
             aq = sb.tile([P, P], U32, name="aq%d" % n, tag="aq%d" % n, align_bytes=64)
             asc = sb.tile([P, P], U8, name="asc%d" % n, align_bytes=64)
-            nc.vector.quantize_mx(out=aq[:].bitcast(FP8X4), scales=asc[:], in_=a_in[:, cols, :].rearrange("p c t -> p (c t)"))
+            nc.vector.quantize_mx(out=aq[:].bitcast(FP8X4), scales=asc[:], in_=a_in[:].rearrange("p c t -> p (c t)"))
             ps = bank(n, "s_ps%d" % n)
             nc.tensor.matmul_mx(out=ps[:], lhsT=aq[:].bitcast(FP8X4), lhsT_scale=asc[:], rhs=w_g[:].bitcast(FP4X4), rhs_scale=sc_g[:], start=True, stop=True)
             s_ps.append(ps)
+
+        njs = sb.tile([P, PACK], F32, name="njs")
+        nc.scalar.activation(njs[:], js_col, ACT.Copy, scale=-1.0)
+        fade_ps = bank(3, "fade_ps")
+        nc.tensor.transpose(fade_ps[:, 0:P], fade_rows, ident[:])
+        fade_col = sb.tile([P, T // P], F32, name="fade_col")
+        nc.scalar.copy(fade_col[:], fade_ps[:, 0 : T // P])
 
         b_raw = []
         for h in range(2):
@@ -132,7 +132,7 @@ def tile_attend_bpairlink_x_kernel(tc, taba, tabb_words, tabb_scales, pw, js, br
             old_sb.extend([t[:, 0, :], t[:, 1, :]])
 
         g = [sb.tile([P, J], F32, name="g%d" % n) for n in range(2)]
-        s = [sb.tile([P, J], F32, name="s%d" % n) for n in range(2)]
+        s = [sb.tile([P, J], F32, name="s%d" % n, tag="s%d" % n, align_bytes=64) for n in range(2)]
         sq = [sb.tile([P, J], F32, name="sq%d" % n) for n in range(2)]
         halves = [(slice(256 * u, 256 * (u + 1)), o3[:, 16 * u : 16 * (u + 1)]) for u in range(2)]
 
@@ -172,11 +172,14 @@ def tile_attend_bpairlink_x_kernel(tc, taba, tabb_words, tabb_scales, pw, js, br
         gq = sb.tile([P, I], U32, name="gq", align_bytes=64)
         gsc = sb.tile([P, I], U8, name="gsc", align_bytes=64)
 
-        def scale_round(n, ps, g_both):
-            g_in = g_both[:, P * n : P * (n + 1), :]
-            nc.vector.tensor_tensor(g_in, quarters(ps[:]).rearrange("p t c -> p c t"), njs[:].unsqueeze(1).to_broadcast([P, P, PACK]), ALU.mult)
+        def scale_round(n, ps, tag):
+            g_in = sb.tile([P, P, PACK], BF16, name="g_in%d" % n, tag=tag, align_bytes=64)
+            nc.vector.tensor_tensor(g_in[:], quarters(ps[:]).rearrange("p t c -> p c t"), njs[:].unsqueeze(1).to_broadcast([P, P, PACK]), ALU.mult)
+            return g_in
+
+        def quantise_gradient(n, g_in):
             cols = slice(P * n, P * (n + 1))
-            nc.vector.quantize_mx(out=gq[:, cols].bitcast(FP8X4), scales=gsc[:, cols], in_=g_in.rearrange("p c t -> p (c t)"))
+            nc.vector.quantize_mx(out=gq[:, cols].bitcast(FP8X4), scales=gsc[:, cols], in_=g_in[:].rearrange("p c t -> p (c t)"))
 
         def quantise(name, src, width):
             q = sb.tile([P, width], U32, name=name + "q", align_bytes=64)
@@ -192,8 +195,8 @@ def tile_attend_bpairlink_x_kernel(tc, taba, tabb_words, tabb_scales, pw, js, br
                 nc.scalar.activation(values[:, cols, :], b_raw[h][:, :, cols].rearrange("p e u -> p u e"), ACT.Copy)
             return pair
 
-        def gather_words(h, pair):
-            words = sb.tile([P, J], F32, name="bw%d" % h)
+        def gather_words(h, pair, tag):
+            words = sb.tile([P, J], F32, name="bw%d" % h, tag=tag, align_bytes=64)
             nc.vector.tensor_copy(words[:], pair[:].indirect(o2[:]))
             return words
 
@@ -205,63 +208,83 @@ def tile_attend_bpairlink_x_kernel(tc, taba, tabb_words, tabb_scales, pw, js, br
             nc.scalar.copy(b_in[:], quarters(ps[:].bitcast(BF16)).rearrange("p t c -> p c t"))
             return b_in
 
-        def product(h, bq, where):
-            ps = bank(where, "gx_ps%d" % h)
+        def product(name, bq, i_cols, where):
+            width = i_cols.stop - i_cols.start
+            ps = bank(where, "gx_ps" + name)
             q, sc = bq
             gx = []
             for e in range(2):
                 cols = slice(P * e, P * (e + 1))
-                nc.tensor.matmul_mx(out=ps[:, I * e : I * (e + 1)], lhsT=q[:, cols].bitcast(FP8X4), lhsT_scale=sc[:, cols],
-                                    rhs=gq[:].bitcast(FP8X4), rhs_scale=gsc[:], start=True, stop=True)
+                nc.tensor.matmul_mx(out=ps[:, width * e : width * (e + 1)], lhsT=q[:, cols].bitcast(FP8X4), lhsT_scale=sc[:, cols],
+                                    rhs=gq[:, i_cols].bitcast(FP8X4), rhs_scale=gsc[:, i_cols], start=True, stop=True)
             for e in range(2):
-                part = sb.tile([P, I], F32, name="gx%d_%d" % (h, e))
-                nc.scalar.copy(part[:], ps[:, I * e : I * (e + 1)])
+                part = sb.tile([P, width], F32, name="gx%s_%d" % (name, e))
+                nc.scalar.copy(part[:], ps[:, width * e : width * (e + 1)])
                 gx.append(part)
             return gx
 
-        def finish(k, gx, banks, tags):
-            nc.vector.tensor_copy(gf[k][:].indirect(o1[:]), gx[:])
+        def put(k, gx, i_cols):
+            nc.vector.tensor_copy(gf[k][:].indirect(o1[:, i_cols.start // 16 : i_cols.stop // 16]), gx[:])
+
+        def finish(k, banks, pieces):
             for u in range(2):
                 ps = bank(banks[u], "back%d_%d" % (k, u))
                 for c in range(4):
                     nc.tensor.transpose(ps[:, P * c : P * (c + 1)], faded[4 * u + c][:, P * k : P * (k + 1)], ident[:])
-                res = sb.tile([P, BANK], F32, name="res%d_%d" % (k, u), tag=tags[u], align_bytes=64)
-                cols = slice(BANK * u, BANK * (u + 1))
-                nc.vector.tensor_tensor(res[:], ps[:], gf[k][:, cols], ALU.add)
-                nc.sync.dma_start(out[P * k : P * (k + 1), cols], res[:])
-
-        sigmoid(0)
-        scores_out(0)
-        square(0)
-        pair0 = cast_pair(0, "aq1")
-        sigmoid(1)
-        pair1 = cast_pair(1, "pair1")
-        scores_out(1)
-        square(1)
-
-        a0 = linked(0, "a_term0")
-        b0 = slope_term(0, placed(0, "s1_0"), "b_term0")
-        gs0 = turn(0, a0, b0, 2)
-        b_in0 = turn_words(0, gather_words(0, pair0), 4)
-        a1 = linked(1, "aq1")
-        b_in1 = turn_words(1, gather_words(1, pair1), 5)
-        bq0 = quantise("b0", b_in0, 2 * P)
-        b1 = slope_term(1, placed(1, "pair1"), "b_term1")
-        gs1 = turn(1, a1, b1, 3)
-        g_both = sb.tile([P, I, PACK], BF16, name="g_both", tag="pair1", align_bytes=64)
-        scale_round(0, gs0, g_both)
-        bq1 = quantise("b1", b_in1, 2 * P)
-        scale_round(1, gs1, g_both)
-        gx = product(0, bq0, 4) + product(1, bq1, 5)
+                width = BANK // pieces[u]
+                for v in range(pieces[u]):
+                    res = sb.tile([P, width], F32, name="res%d_%d_%d" % (k, u, v))
+                    cols = slice(BANK * u + width * v, BANK * u + width * (v + 1))
+                    nc.vector.tensor_tensor(res[:], ps[:, width * v : width * (v + 1)], gf[k][:, cols], ALU.add)
+                    nc.sync.dma_start(out[P * k : P * (k + 1), cols], res[:])
 
         faded = []
-        for c in range(T // P):
-            ps = bank((6, 7, 0, 1)[c % 4], "old_ps%d" % c)
+
+        def fade_block(c, where):
+            ps = bank(where, "old_ps%d" % c)
             for k in range(4):
                 nc.tensor.transpose(ps[:, P * k : P * (k + 1)], old_sb[k][:, P * c : P * (c + 1)], ident[:])
             f = sb.tile([P, D], F32, name="faded%d" % c)
             nc.scalar.activation(f[:], ps[:], ACT.Copy, scale=fade_col[:, c : c + 1])
             faded.append(f)
 
-        for k in range(4):
-            finish(k, gx[k], ((6, 7), (0, 1), (2, 3), (4, 5))[k], ("res%d_0" % k, "res%d_1" % k))
+        first, second, both = slice(0, P), slice(P, I), slice(0, I)
+        sigmoid(0)
+        scores_out(0)
+        sigmoid(1)
+        square(0)
+        pair0 = cast_pair(0, "aq1")
+        scores_out(1)
+        pair1 = cast_pair(1, "pair1")
+        square(1)
+
+        a0 = linked(0, "a_term0")
+        s1_0 = placed(0, "s1_0")
+        a1 = linked(1, "a_term1")
+        b0 = slope_term(0, s1_0, "b_term0")
+        gs0 = turn(0, a0, b0, 2)
+        b_in0 = turn_words(0, gather_words(0, pair0, "bw0"), 4)
+        s1_1 = placed(1, "aq1")
+        g_in0 = scale_round(0, gs0, "s1")
+        bq0 = quantise("b0", b_in0, 2 * P)
+        quantise_gradient(0, g_in0)
+        b1 = slope_term(1, s1_1, "b_in0")
+        gs1 = turn(1, a1, b1, 3)
+        b_in1 = turn_words(1, gather_words(1, pair1, "aq1"), 5)
+        gx_first = product("a", bq0, first, 2)
+        put(0, gx_first[0], first)
+        put(1, gx_first[1], first)
+        quantise_gradient(1, scale_round(1, gs1, "g_in1"))
+        bq1 = quantise("b1", b_in1, 2 * P)
+        gx_second = product("b", bq0, second, 3)
+        gx_both = product("c", bq1, both, 4)
+        for c in range(8):
+            fade_block(c, (6, 7, 0, 1)[c % 4])
+        put(0, gx_second[0], second)
+        put(1, gx_second[1], second)
+        finish(0, (2, 5), (1, 1))
+        finish(1, (6, 7), (1, 1))
+        put(2, gx_both[0], both)
+        put(3, gx_both[1], both)
+        finish(2, (0, 1), (1, 1))
+        finish(3, (3, 4), (1, 2))

@@ -21,6 +21,7 @@ P = 128
 PACK = 4
 BANK = 512
 S1_WINDOW = 704
+G_WINDOW = 528
 
 
 def tile_attend_bpairlink_x_kernel(tc, taba, tabb_words, tabb_scales, pw, js, brows, old, fade, offs3, offs, offs2, out):
@@ -40,11 +41,11 @@ def tile_attend_bpairlink_x_kernel(tc, taba, tabb_words, tabb_scales, pw, js, br
         o1 = lists.tile([P, I // 16], U16, name="o1")
         o3 = lists.tile([P, J // 16], U16, name="o3")
 
-        zero = sb.tile([P, 1], F32, name="zero", tag="old0")
+        zero = sb.tile([P, 1], F32, name="zero", tag="b_raw1", align_bytes=64)
         nc.vector.memset(zero[:], 0.0)
         sc_win = sb.tile([P, U], U8, name="sc_win", tag="a_in", align_bytes=64)
         nc.vector.memset(sc_win[:].bitcast(I32), 0)
-        pw_col = sb.tile([P, PACK], F32, name="pw_col", tag="b_raw0")
+        pw_col = sb.tile([P, PACK], F32, name="pw_col", tag="b_raw0", align_bytes=64)
         nc.scalar.dma_start(pw_col[:], pw.rearrange("o (p t) -> (o p) t", t=PACK))
         half = sb.tile([P, 1], F32, name="half")
         nc.scalar.activation(half[:], zero[:], ACT.Sigmoid)
@@ -54,12 +55,12 @@ def tile_attend_bpairlink_x_kernel(tc, taba, tabb_words, tabb_scales, pw, js, br
         nc.sync.dma_start(w_win[:].bitcast(I32), tabb_words[0].bitcast(I32))
         nc.sync.dma_start(o1[:], offs)
         a_rows = taba.rearrange("(p t) c -> p t c", t=PACK)
-        a01 = sb.tile([P, 2, T], F32, name="a01", tag="b_raw1")
+        a01 = sb.tile([P, 2, T], F32, name="a01", tag="old0", align_bytes=64)
         nc.sync.dma_start(a01[:], a_rows[:, 0:2, :])
         for q in range(4):
             nc.sync.dma_start(sc_win[32 * q : 32 * q + 4, :].bitcast(I32), tabb_scales[0, 4 * q : 4 * q + 4, :].bitcast(I32))
         nc.sync.dma_start(o3[:], offs3)
-        a23 = sb.tile([P, 2, T], F32, name="a23", tag="old0")
+        a23 = sb.tile([P, 2, T], F32, name="a23", tag="b_raw1", align_bytes=64)
         a2, a3 = a23[:, 0, :], a23[:, 1, :]
         nc.sync.dma_start(a2, a_rows[:, 2, :])
         nc.sync.dma_start(a3, a_rows[:, 3, :])
@@ -93,7 +94,7 @@ def tile_attend_bpairlink_x_kernel(tc, taba, tabb_words, tabb_scales, pw, js, br
         js_col = small[:, P : P + PACK]
         nc.sync.dma_start(small[0 : T // P, 0:P], fade.rearrange("o (c p) -> (o c) p", p=P))
         nc.sync.dma_start(js_col, js.rearrange("o (p t) -> (o p) t", t=PACK))
-        a_pair = sb.tile([P, T], U32, name="a_pair", tag="old1")
+        a_pair = sb.tile([P, T], U32, name="a_pair", tag="old1", align_bytes=64)
         a_pair_values = a_pair[:].bitcast(BF16).rearrange("p (c e) -> p c e", e=2)
         nc.scalar.activation(a_pair_values, a01[:].rearrange("p e c -> p c e"), ACT.Copy)
         s_ps = []
@@ -111,44 +112,47 @@ def tile_attend_bpairlink_x_kernel(tc, taba, tabb_words, tabb_scales, pw, js, br
             nc.tensor.matmul_mx(out=ps[:], lhsT=aq[:].bitcast(FP8X4), lhsT_scale=asc[:], rhs=w_g[:].bitcast(FP4X4), rhs_scale=sc_g[:], start=True, stop=True)
             s_ps.append(ps)
 
-        njs = sb.tile([P, PACK], F32, name="njs")
+        njs = sb.tile([P, PACK], F32, name="njs", tag="njs", align_bytes=64)
         nc.scalar.activation(njs[:], js_col, ACT.Copy, scale=-1.0)
         fade_ps = bank(3, "fade_ps")
         nc.tensor.transpose(fade_ps[:, 0:P], fade_rows, ident[:])
         fade_col = sb.tile([P, T // P], F32, name="fade_col")
         nc.scalar.copy(fade_col[:], fade_ps[:, 0 : T // P])
 
-        b_raw = []
-        for h in range(2):
-            t = sb.tile([P, 2, U], F32, name="b_raw%d" % h, tag="b_raw%d" % h)
+        def load_brows(h):
+            t = sb.tile([P, 2, U], F32, name="b_raw%d" % h, tag="b_raw%d" % h, align_bytes=64)
             nc.sync.dma_start(t[:], brows[256 * h : 256 * (h + 1), :].rearrange("(p e) u -> p e u", e=2))
-            b_raw.append(t)
+            return t
 
-        old_rows = old.rearrange("(k p) t -> p k t", p=P)
-        old_sb = []
-        for h in range(2):
-            t = sb.tile([P, 2, T], F32, name="old%d" % h, tag="old%d" % h)
-            nc.sync.dma_start(t[:], old_rows[:, 2 * h : 2 * h + 2, :])
-            old_sb.extend([t[:, 0, :], t[:, 1, :]])
+        def load_old(u):
+            t = sb.tile([P, 4, BANK], F32, name="old%d" % u, tag="old%d" % u, align_bytes=64)
+            nc.sync.dma_start(t[:], old.rearrange("(k p) t -> p k t", p=P)[:, :, BANK * u : BANK * (u + 1)])
+            return t
 
-        g = [sb.tile([P, J], F32, name="g%d" % n) for n in range(2)]
-        s = [sb.tile([P, J], F32, name="s%d" % n, tag="s%d" % n, align_bytes=64) for n in range(2)]
+        b_raw = [load_brows(0)]
+        old_sb = [load_old(0)]
+        b_raw.append(load_brows(1))
+        old_sb.append(load_old(1))
+
+        g = [sb.tile([P, G_WINDOW], F32, name="g%d" % n, tag="g%d" % n, align_bytes=64) for n in range(2)]
+        for n in range(2):
+            nc.gpsimd.memset(g[n][:, J:G_WINDOW], 0.0)
+        s = []
         sq = [sb.tile([P, J], F32, name="sq%d" % n) for n in range(2)]
-        halves = [(slice(256 * u, 256 * (u + 1)), o3[:, 16 * u : 16 * (u + 1)]) for u in range(2)]
 
         def sigmoid(n):
-            nc.scalar.activation(g[n][:], s_ps[n][:], ACT.Sigmoid)
+            nc.scalar.activation(g[n][:, 0:J], s_ps[n][:], ACT.Sigmoid)
 
         def scores_out(n):
+            s.append(sb.tile([P, J], F32, name="s%d" % n, tag=("s0", "b_raw0")[n], align_bytes=64))
             nc.scalar.copy(s[n][:], s_ps[n][:])
 
         def square(n):
-            nc.scalar.activation(sq[n][:], g[n][:], ACT.Square, bias=half[:], scale=-1.0)
+            nc.scalar.activation(sq[n][:], g[n][:, 0:J], ACT.Square, bias=half[:], scale=-1.0)
 
         def linked(n, tag):
             a_term = sb.tile([P, J], F32, name="a_term%d" % n, tag=tag, align_bytes=64)
-            for cols, lst in halves:
-                nc.vector.tensor_tensor(a_term[:, cols], g[n][:].indirect(lst), npw_b[:, cols], ALU.mult)
+            nc.vector.tensor_tensor(a_term[:], g[n][:].indirect(o3[:]), npw_b[:], ALU.mult)
             return a_term
 
         def placed(n, tag):
@@ -182,18 +186,15 @@ def tile_attend_bpairlink_x_kernel(tc, taba, tabb_words, tabb_scales, pw, js, br
             nc.vector.quantize_mx(out=gq[:, cols].bitcast(FP8X4), scales=gsc[:, cols], in_=g_in[:].rearrange("p c t -> p (c t)"))
 
         def quantise(name, src, width):
-            q = sb.tile([P, width], U32, name=name + "q", align_bytes=64)
+            q = sb.tile([P, width], U32, name=name + "q", tag=name + "q", align_bytes=64)
             sc = sb.tile([P, width], U8, name=name + "s", align_bytes=64)
             nc.vector.quantize_mx(out=q[:].bitcast(FP8X4), scales=sc[:], in_=src[:].rearrange("p c t -> p (c t)"))
             return q, sc
 
-        def cast_pair(h, tag):
-            pair = sb.tile([P, U], F32, name="pair%d" % h, tag=tag, align_bytes=64)
+        def cast_half(h, pair, u):
             values = pair[:].bitcast(BF16).rearrange("p (u e) -> p u e", e=2)
-            for u in range(2):
-                cols = slice(512 * u, 512 * (u + 1))
-                nc.scalar.activation(values[:, cols, :], b_raw[h][:, :, cols].rearrange("p e u -> p u e"), ACT.Copy)
-            return pair
+            cols = slice(512 * u, 512 * (u + 1))
+            nc.scalar.activation(values[:, cols, :], b_raw[h][:, :, cols].rearrange("p e u -> p u e"), ACT.Copy)
 
         def gather_words(h, pair, tag):
             words = sb.tile([P, J], F32, name="bw%d" % h, tag=tag, align_bytes=64)
@@ -208,23 +209,20 @@ def tile_attend_bpairlink_x_kernel(tc, taba, tabb_words, tabb_scales, pw, js, br
             nc.scalar.copy(b_in[:], quarters(ps[:].bitcast(BF16)).rearrange("p t c -> p c t"))
             return b_in
 
-        def product(name, bq, i_cols, where):
+        def product(name, bq, i_cols, where, tag):
             width = i_cols.stop - i_cols.start
             ps = bank(where, "gx_ps" + name)
             q, sc = bq
-            gx = []
             for e in range(2):
                 cols = slice(P * e, P * (e + 1))
                 nc.tensor.matmul_mx(out=ps[:, width * e : width * (e + 1)], lhsT=q[:, cols].bitcast(FP8X4), lhsT_scale=sc[:, cols],
                                     rhs=gq[:, i_cols].bitcast(FP8X4), rhs_scale=gsc[:, i_cols], start=True, stop=True)
-            for e in range(2):
-                part = sb.tile([P, width], F32, name="gx%s_%d" % (name, e))
-                nc.scalar.copy(part[:], ps[:, width * e : width * (e + 1)])
-                gx.append(part)
-            return gx
+            gx = sb.tile([P, 2 * width], F32, name="gx" + name, tag=tag, align_bytes=64)
+            nc.scalar.copy(gx[:], ps[:, 0 : 2 * width])
+            return [gx[:, 0:width], gx[:, width : 2 * width]]
 
         def put(k, gx, i_cols):
-            nc.vector.tensor_copy(gf[k][:].indirect(o1[:, i_cols.start // 16 : i_cols.stop // 16]), gx[:])
+            nc.vector.tensor_copy(gf[k][:].indirect(o1[:, i_cols.start // 16 : i_cols.stop // 16]), gx)
 
         def finish(k, banks, pieces):
             for u in range(2):
@@ -238,53 +236,80 @@ def tile_attend_bpairlink_x_kernel(tc, taba, tabb_words, tabb_scales, pw, js, br
                     nc.vector.tensor_tensor(res[:], ps[:, width * v : width * (v + 1)], gf[k][:, cols], ALU.add)
                     nc.sync.dma_start(out[P * k : P * (k + 1), cols], res[:])
 
+        def finish_on_tensor(k, turn_banks, banks, tags):
+            turned = []
+            for u in range(2):
+                ps = bank(turn_banks[u], "gf_ps%d_%d" % (k, u))
+                for c in range(4):
+                    nc.tensor.transpose(ps[:, P * c : P * (c + 1)], gf[k][:, BANK * u + P * c : BANK * u + P * (c + 1)], ident[:])
+                t = sb.tile([P, BANK], F32, name="gf_t%d_%d" % (k, u))
+                nc.scalar.copy(t[:], ps[:])
+                turned.append(t)
+            for u in range(2):
+                ps = bank(banks[u], "back%d_%d" % (k, u))
+                for c in range(4):
+                    nc.tensor.matmul(ps[:, P * c : P * (c + 1)], lhsT=faded[4 * u + c][:, P * k : P * (k + 1)], rhs=ident[:], is_transpose=True,
+                                     start=(c == 0), stop=False)
+                for c in range(4):
+                    nc.tensor.matmul(ps[:, P * c : P * (c + 1)], lhsT=turned[u][:, P * c : P * (c + 1)], rhs=ident[:], is_transpose=True,
+                                     start=False, stop=(c == 3))
+                res = sb.tile([P, BANK], F32, name="res%d_%d" % (k, u), tag=tags[u], align_bytes=64)
+                nc.scalar.copy(res[:], ps[:])
+                nc.scalar.dma_start(out[P * k : P * (k + 1), BANK * u : BANK * (u + 1)], res[:])
+
         faded = []
 
         def fade_block(c, where):
             ps = bank(where, "old_ps%d" % c)
             for k in range(4):
-                nc.tensor.transpose(ps[:, P * k : P * (k + 1)], old_sb[k][:, P * c : P * (c + 1)], ident[:])
+                nc.tensor.transpose(ps[:, P * k : P * (k + 1)], old_sb[c // 4][:, k, P * (c % 4) : P * (c % 4 + 1)], ident[:])
             f = sb.tile([P, D], F32, name="faded%d" % c)
             nc.scalar.activation(f[:], ps[:], ACT.Copy, scale=fade_col[:, c : c + 1])
             faded.append(f)
 
         first, second, both = slice(0, P), slice(P, I), slice(0, I)
+        old_banks = (4, 5, 6, 7, 3, 1, 6, 5)
+        pair = [sb.tile([P, U], F32, name="pair%d" % h, tag=("aq1", "pair1")[h], align_bytes=64) for h in range(2)]
         sigmoid(0)
         scores_out(0)
         sigmoid(1)
         square(0)
-        pair0 = cast_pair(0, "aq1")
+        cast_half(0, pair[0], 0)
+        cast_half(0, pair[0], 1)
         scores_out(1)
-        pair1 = cast_pair(1, "pair1")
         square(1)
+        for c in range(4):
+            fade_block(c, old_banks[c])
+        cast_half(1, pair[1], 0)
 
         a0 = linked(0, "a_term0")
         s1_0 = placed(0, "s1_0")
         a1 = linked(1, "a_term1")
-        b0 = slope_term(0, s1_0, "b_term0")
+        b0 = slope_term(0, s1_0, "old0")
         gs0 = turn(0, a0, b0, 2)
-        b_in0 = turn_words(0, gather_words(0, pair0, "bw0"), 4)
-        s1_1 = placed(1, "aq1")
-        g_in0 = scale_round(0, gs0, "s1")
-        bq0 = quantise("b0", b_in0, 2 * P)
+        b_in0 = turn_words(0, gather_words(0, pair[0], "bw0"), 4)
+        cast_half(1, pair[1], 1)
+        s1_1 = placed(1, "s1_0")
+        g_in0 = scale_round(0, gs0, "g1")
+        b1 = slope_term(1, s1_1, "b_term1")
+        gs1 = turn(1, a1, b1, 5)
         quantise_gradient(0, g_in0)
-        b1 = slope_term(1, s1_1, "b_in0")
-        gs1 = turn(1, a1, b1, 3)
-        b_in1 = turn_words(1, gather_words(1, pair1, "aq1"), 5)
-        gx_first = product("a", bq0, first, 2)
+        bq0 = quantise("b0", b_in0, 2 * P)
+        b_in1 = turn_words(1, gather_words(1, pair[1], "bw1"), 4)
+        quantise_gradient(1, scale_round(1, gs1, "b_raw1"))
+        gx_first = product("a", bq0, first, 6, "njs")
+        gx_second = product("b", bq0, second, 2, "gxb")
         put(0, gx_first[0], first)
         put(1, gx_first[1], first)
-        quantise_gradient(1, scale_round(1, gs1, "g_in1"))
-        bq1 = quantise("b1", b_in1, 2 * P)
-        gx_second = product("b", bq0, second, 3)
-        gx_both = product("c", bq1, both, 4)
-        for c in range(8):
-            fade_block(c, (6, 7, 0, 1)[c % 4])
         put(0, gx_second[0], second)
         put(1, gx_second[1], second)
-        finish(0, (2, 5), (1, 1))
-        finish(1, (6, 7), (1, 1))
+        bq1 = quantise("b1", b_in1, 2 * P)
+        gx_both = product("c", bq1, both, 4, "gxc")
+        for c in range(4, 8):
+            fade_block(c, old_banks[c])
+        finish_on_tensor(0, (2, 1), (0, 7), ("res00", "res01"))
+        finish(1, (3, 6), (1, 1))
         put(2, gx_both[0], both)
         put(3, gx_both[1], both)
-        finish(2, (0, 1), (1, 1))
-        finish(3, (3, 4), (1, 2))
+        finish(2, (5, 4), (1, 1))
+        finish(3, (2, 1), (1, 2))

@@ -224,38 +224,33 @@ def tile_attend_bpairlink_x_kernel(tc, taba, tabb_words, tabb_scales, pw, js, br
         def put(k, gx, i_cols):
             nc.vector.tensor_copy(gf[k][:].indirect(o1[:, i_cols.start // 16 : i_cols.stop // 16]), gx)
 
-        def finish(k, banks, pieces):
-            for u in range(2):
-                ps = bank(banks[u], "back%d_%d" % (k, u))
-                for c in range(4):
-                    nc.tensor.transpose(ps[:, P * c : P * (c + 1)], faded[4 * u + c][:, P * k : P * (k + 1)], ident[:])
-                width = BANK // pieces[u]
-                for v in range(pieces[u]):
-                    res = sb.tile([P, width], F32, name="res%d_%d_%d" % (k, u, v))
-                    cols = slice(BANK * u + width * v, BANK * u + width * (v + 1))
-                    nc.vector.tensor_tensor(res[:], ps[:, width * v : width * (v + 1)], gf[k][:, cols], ALU.add)
-                    nc.sync.dma_start(out[P * k : P * (k + 1), cols], res[:])
+        def turn_faded(ps, k, u, closed):
+            for c in range(4):
+                nc.tensor.matmul(ps[:, P * c : P * (c + 1)], lhsT=faded[4 * u + c][:, P * k : P * (k + 1)], rhs=ident[:], is_transpose=True,
+                                 start=(c == 0), stop=(closed and c == 3))
 
-        def finish_on_tensor(k, turn_banks, banks, tags):
-            turned = []
-            for u in range(2):
-                ps = bank(turn_banks[u], "gf_ps%d_%d" % (k, u))
-                for c in range(4):
-                    nc.tensor.transpose(ps[:, P * c : P * (c + 1)], gf[k][:, BANK * u + P * c : BANK * u + P * (c + 1)], ident[:])
-                t = sb.tile([P, BANK], F32, name="gf_t%d_%d" % (k, u))
-                nc.scalar.copy(t[:], ps[:])
-                turned.append(t)
-            for u in range(2):
-                ps = bank(banks[u], "back%d_%d" % (k, u))
-                for c in range(4):
-                    nc.tensor.matmul(ps[:, P * c : P * (c + 1)], lhsT=faded[4 * u + c][:, P * k : P * (k + 1)], rhs=ident[:], is_transpose=True,
-                                     start=(c == 0), stop=False)
-                for c in range(4):
-                    nc.tensor.matmul(ps[:, P * c : P * (c + 1)], lhsT=turned[u][:, P * c : P * (c + 1)], rhs=ident[:], is_transpose=True,
-                                     start=False, stop=(c == 3))
-                res = sb.tile([P, BANK], F32, name="res%d_%d" % (k, u), tag=tags[u], align_bytes=64)
-                nc.scalar.copy(res[:], ps[:])
-                nc.scalar.dma_start(out[P * k : P * (k + 1), BANK * u : BANK * (u + 1)], res[:])
+        def finish(k, u, where, pieces):
+            ps = bank(where, "back%d_%d" % (k, u))
+            turn_faded(ps, k, u, True)
+            width = BANK // pieces
+            for v in range(pieces):
+                res = sb.tile([P, width], F32, name="res%d_%d_%d" % (k, u, v))
+                cols = slice(BANK * u + width * v, BANK * u + width * (v + 1))
+                nc.vector.tensor_tensor(res[:], ps[:, width * v : width * (v + 1)], gf[k][:, cols], ALU.add)
+                nc.sync.dma_start(out[P * k : P * (k + 1), cols], res[:])
+
+        def faded_rows(k, u, where):
+            ps = bank(where, "back%d_%d" % (k, u))
+            turn_faded(ps, k, u, True)
+            t = sb.tile([P, BANK], F32, name="faded_rows%d_%d" % (k, u))
+            nc.scalar.copy(t[:], ps[:])
+            return t
+
+        def finish_on_gpsimd(k, u, rows):
+            res = sb.tile([P, BANK], F32, name="res%d_%d" % (k, u))
+            cols = slice(BANK * u, BANK * (u + 1))
+            nc.gpsimd.tensor_tensor(res[:], rows[:], gf[k][:, cols], ALU.add)
+            nc.sync.dma_start(out[P * k : P * (k + 1), cols], res[:])
 
         faded = []
 
@@ -295,9 +290,10 @@ def tile_attend_bpairlink_x_kernel(tc, taba, tabb_words, tabb_scales, pw, js, br
         gs1 = turn(1, a1, b1, 5)
         quantise_gradient(0, g_in0)
         bq0 = quantise("b0", b_in0, 2 * P)
-        b_in1 = turn_words(1, gather_words(1, pair[1], "bw1"), 4)
+        words1 = gather_words(1, pair[1], "bw1")
         quantise_gradient(1, scale_round(1, gs1, "b_raw1"))
         gx_first = product("a", bq0, first, 6, "njs")
+        b_in1 = turn_words(1, words1, 4)
         gx_second = product("b", bq0, second, 2, "gxb")
         put(0, gx_first[0], first)
         put(1, gx_first[1], first)
@@ -305,11 +301,14 @@ def tile_attend_bpairlink_x_kernel(tc, taba, tabb_words, tabb_scales, pw, js, br
         put(1, gx_second[1], second)
         bq1 = quantise("b1", b_in1, 2 * P)
         gx_both = product("c", bq1, both, 4, "gxc")
+        rows = [faded_rows(k, 0, (0, 7, 3, 1)[k]) for k in range(4)]
         for c in range(4, 8):
             fade_block(c, old_banks[c])
-        finish_on_tensor(0, (2, 1), (0, 7), ("res00", "res01"))
-        finish(1, (3, 6), (1, 1))
+        finish_on_gpsimd(0, 0, rows[0])
+        finish_on_gpsimd(1, 0, rows[1])
         put(2, gx_both[0], both)
+        finish_on_gpsimd(2, 0, rows[2])
         put(3, gx_both[1], both)
-        finish(2, (5, 4), (1, 1))
-        finish(3, (2, 1), (1, 2))
+        finish_on_gpsimd(3, 0, rows[3])
+        for k in range(4):
+            finish(k, 1, (0, 7, 2, 3)[k], 2 if k == 3 else 1)

from contextlib import ExitStack

import concourse.mybir as mybir
from concourse.masks import make_identity

D, T, U, I, J = 512, 1024, 1024, 256, 512
FLOPS = 2 * D * I * J * 2

F32 = mybir.dt.float32
BF16 = mybir.dt.bfloat16
I32 = mybir.dt.int32
U32 = mybir.dt.uint32
U16 = mybir.dt.uint16
U8 = mybir.dt.uint8
FP8X4 = mybir.dt.float8_e4m3fn_x4
FP4X4 = mybir.dt.float4_e2m1fn_x4
ACT = mybir.ActivationFunctionType
ALU = mybir.AluOpType

P = 128
PACK = 4
BANK = 512
S1_WINDOW = 704
G_WINDOW = 528


def tile_attend_bpairlink_x_kernel(tc, taba, tabb_words, tabb_scales, pw, js, brows, old, fade, offs3, offs, offs2, out):
    nc = tc.nc
    with ExitStack() as ctx:
        lists = ctx.enter_context(tc.tile_pool(name="lists", bufs=1))
        sb = ctx.enter_context(tc.tile_pool(name="sb", bufs=1))
        psum = ctx.enter_context(tc.psum_pool(name="psum", bufs=1))

        def bank(n, name):
            return psum.tile([P, BANK], F32, name=name, tag="bank%d" % n)

        def quarters(ap):
            return ap.rearrange("p (t c) -> p t c", t=PACK)

        o2 = lists.tile([P, J // 16], U16, name="o2")
        o1 = lists.tile([P, I // 16], U16, name="o1")
        o3 = lists.tile([P, J // 16], U16, name="o3")

        zero = sb.tile([P, 1], F32, name="zero", tag="b_raw1", align_bytes=64)
        nc.vector.memset(zero[:], 0.0)
        sc_win = sb.tile([P, U], U8, name="sc_win", tag="a_in", align_bytes=64)
        nc.vector.memset(sc_win[:].bitcast(I32), 0)
        pw_col = sb.tile([P, PACK], F32, name="pw_col", tag="b_raw0", align_bytes=64)
        nc.scalar.dma_start(pw_col[:], pw.rearrange("o (p t) -> (o p) t", t=PACK))
        half = sb.tile([P, 1], F32, name="half")
        nc.scalar.activation(half[:], zero[:], ACT.Sigmoid)

        nc.sync.dma_start(o2[:], offs2)
        w_win = sb.tile([P, U], U16, name="w_win", tag="small")
        nc.sync.dma_start(w_win[:].bitcast(I32), tabb_words[0].bitcast(I32))
        nc.sync.dma_start(o1[:], offs)
        a_rows = taba.rearrange("(p t) c -> p t c", t=PACK)
        a01 = sb.tile([P, 2, T], F32, name="a01", tag="old0", align_bytes=64)
        nc.sync.dma_start(a01[:], a_rows[:, 0:2, :])
        for q in range(4):
            nc.sync.dma_start(sc_win[32 * q : 32 * q + 4, :].bitcast(I32), tabb_scales[0, 4 * q : 4 * q + 4, :].bitcast(I32))
        nc.sync.dma_start(o3[:], offs3)
        a23 = sb.tile([P, 2, T], F32, name="a23", tag="b_raw1", align_bytes=64)
        a2, a3 = a23[:, 0, :], a23[:, 1, :]
        nc.sync.dma_start(a2, a_rows[:, 2, :])
        nc.sync.dma_start(a3, a_rows[:, 3, :])

        ident = sb.tile([P, P], F32, name="ident")
        make_identity(nc, ident[:])

        gf = []
        for k in range(4):
            t = sb.tile([P, T], F32, name="gf%d" % k)
            nc.vector.memset(t[:], 0.0)
            gf.append(t)

        pw_ps = bank(2, "pw_ps")
        for t in range(PACK):
            nc.tensor.transpose(pw_ps[:, P * t : P * (t + 1)], pw_col[:, t : t + 1].to_broadcast([P, P]), ident[:])
        pw_b = sb.tile([P, J], F32, name="pw_b")
        npw_b = sb.tile([P, J], F32, name="npw_b")
        pw_nat = quarters(pw_ps[:]).rearrange("p t c -> p c t")
        nc.scalar.activation(npw_b[:].rearrange("p (c t) -> p c t", t=PACK), pw_nat, ACT.Copy, scale=-1.0)
        nc.scalar.activation(pw_b[:].rearrange("p (c t) -> p c t", t=PACK), pw_nat, ACT.Copy)

        w_g = sb.tile([P, J], U16, name="w_g", align_bytes=64)
        nc.vector.tensor_copy(w_g[:], w_win[:].indirect(o2[:]))
        sc_g = sb.tile([P, J], U8, name="sc_g", align_bytes=64)
        nc.vector.tensor_copy(sc_g[:], sc_win[:].indirect(o2[:]))

        small = sb.tile([P, P + 8], F32, name="small", tag="small")
        nc.vector.memset(small[:], 0.0)
        fade_rows = small[:, 0:P]
        js_col = small[:, P : P + PACK]
        nc.sync.dma_start(small[0 : T // P, 0:P], fade.rearrange("o (c p) -> (o c) p", p=P))
        nc.sync.dma_start(js_col, js.rearrange("o (p t) -> (o p) t", t=PACK))
        a_pair = sb.tile([P, T], U32, name="a_pair", tag="old1", align_bytes=64)
        a_pair_values = a_pair[:].bitcast(BF16).rearrange("p (c e) -> p c e", e=2)
        nc.scalar.activation(a_pair_values, a01[:].rearrange("p e c -> p c e"), ACT.Copy)
        s_ps = []
        for n in range(2):
            a_in = sb.tile([P, P, PACK], BF16, name="a_in%d" % n, tag="a_in", align_bytes=64)
            a_words = a_in[:].rearrange("p c t -> p (c t)").bitcast(U32).rearrange("p (c e) -> p c e", e=2)
            lst = o1[:, 8 * n : 8 * n + 8]
            nc.vector.tensor_copy(a_in[:, :, 2], a2.indirect(lst))
            nc.vector.tensor_copy(a_in[:, :, 3], a3.indirect(lst))
            nc.vector.tensor_copy(a_words[:, :, 0], a_pair[:].indirect(lst))
            aq = sb.tile([P, P], U32, name="aq%d" % n, tag="aq%d" % n, align_bytes=64)
            asc = sb.tile([P, P], U8, name="asc%d" % n, align_bytes=64)
            nc.vector.quantize_mx(out=aq[:].bitcast(FP8X4), scales=asc[:], in_=a_in[:].rearrange("p c t -> p (c t)"))
            ps = bank(n, "s_ps%d" % n)
            nc.tensor.matmul_mx(out=ps[:], lhsT=aq[:].bitcast(FP8X4), lhsT_scale=asc[:], rhs=w_g[:].bitcast(FP4X4), rhs_scale=sc_g[:], start=True, stop=True)
            s_ps.append(ps)

        njs = sb.tile([P, PACK], F32, name="njs", tag="njs", align_bytes=64)
        nc.scalar.activation(njs[:], js_col, ACT.Copy, scale=-1.0)
        fade_ps = bank(3, "fade_ps")
        nc.tensor.transpose(fade_ps[:, 0:P], fade_rows, ident[:])
        fade_col = sb.tile([P, T // P], F32, name="fade_col")
        nc.scalar.copy(fade_col[:], fade_ps[:, 0 : T // P])

        def load_brows(h):
            t = sb.tile([P, 2, U], F32, name="b_raw%d" % h, tag="b_raw%d" % h, align_bytes=64)
            nc.sync.dma_start(t[:], brows[256 * h : 256 * (h + 1), :].rearrange("(p e) u -> p e u", e=2))
            return t

        def load_old(u):
            t = sb.tile([P, 4, BANK], F32, name="old%d" % u, tag="old%d" % u, align_bytes=64)
            nc.sync.dma_start(t[:], old.rearrange("(k p) t -> p k t", p=P)[:, :, BANK * u : BANK * (u + 1)])
            return t

        b_raw = [load_brows(0)]
        old_sb = [load_old(0)]
        b_raw.append(load_brows(1))
        old_sb.append(load_old(1))

        g = [sb.tile([P, G_WINDOW], F32, name="g%d" % n, tag="g%d" % n, align_bytes=64) for n in range(2)]
        for n in range(2):
            nc.gpsimd.memset(g[n][:, J:G_WINDOW], 0.0)
        s = []
        sq = [sb.tile([P, J], F32, name="sq%d" % n) for n in range(2)]

        def sigmoid(n):
            nc.scalar.activation(g[n][:, 0:J], s_ps[n][:], ACT.Sigmoid)

        def scores_out(n):
            s.append(sb.tile([P, J], F32, name="s%d" % n, tag=("s0", "b_raw0")[n], align_bytes=64))
            nc.scalar.copy(s[n][:], s_ps[n][:])

        def square(n):
            nc.scalar.activation(sq[n][:], g[n][:, 0:J], ACT.Square, bias=half[:], scale=-1.0)

        def linked(n, tag):
            a_term = sb.tile([P, J], F32, name="a_term%d" % n, tag=tag, align_bytes=64)
            nc.vector.tensor_tensor(a_term[:], g[n][:].indirect(o3[:]), npw_b[:], ALU.mult)
            return a_term

        def placed(n, tag):
            s1 = sb.tile([P, S1_WINDOW], F32, name="s1_%d" % n, tag=tag, align_bytes=64)
            nc.vector.tensor_tensor(s1[:].indirect(o3[:]), s[n][:], pw_b[:], ALU.mult)
            return s1

        def slope_term(n, s1, tag):
            b_term = sb.tile([P, J], F32, name="b_term%d" % n, tag=tag, align_bytes=64)
            nc.vector.scalar_tensor_tensor(b_term[:], sq[n][:], 0.25, s1[:, 0:J], ALU.subtract, ALU.mult)
            return b_term

        def turn(n, a_term, b_term, where):
            ps = bank(where, "gs_ps%d" % n)
            for m, term in enumerate((a_term, b_term)):
                for t in range(PACK):
                    nc.tensor.matmul(ps[:, P * t : P * (t + 1)], lhsT=term[:, t : J : PACK], rhs=ident[:], is_transpose=True,
                                     start=(m == 0 and t == 0), stop=(m == 1 and t == PACK - 1))
            return ps

        gq = sb.tile([P, I], U32, name="gq", align_bytes=64)
        gsc = sb.tile([P, I], U8, name="gsc", align_bytes=64)

        def scale_round(n, ps, tag):
            g_in = sb.tile([P, P, PACK], BF16, name="g_in%d" % n, tag=tag, align_bytes=64)
            nc.vector.tensor_tensor(g_in[:], quarters(ps[:]).rearrange("p t c -> p c t"), njs[:].unsqueeze(1).to_broadcast([P, P, PACK]), ALU.mult)
            return g_in

        def quantise_gradient(n, g_in):
            cols = slice(P * n, P * (n + 1))
            nc.vector.quantize_mx(out=gq[:, cols].bitcast(FP8X4), scales=gsc[:, cols], in_=g_in[:].rearrange("p c t -> p (c t)"))

        def quantise(name, src, width):
            q = sb.tile([P, width], U32, name=name + "q", tag=name + "q", align_bytes=64)
            sc = sb.tile([P, width], U8, name=name + "s", align_bytes=64)
            nc.vector.quantize_mx(out=q[:].bitcast(FP8X4), scales=sc[:], in_=src[:].rearrange("p c t -> p (c t)"))
            return q, sc

        def cast_half(h, pair, u):
            values = pair[:].bitcast(BF16).rearrange("p (u e) -> p u e", e=2)
            cols = slice(512 * u, 512 * (u + 1))
            nc.scalar.activation(values[:, cols, :], b_raw[h][:, :, cols].rearrange("p e u -> p u e"), ACT.Copy)

        def gather_words(h, pair, tag):
            words = sb.tile([P, J], F32, name="bw%d" % h, tag=tag, align_bytes=64)
            nc.vector.tensor_copy(words[:], pair[:].indirect(o2[:]))
            return words

        def turn_words(h, words, where):
            ps = bank(where, "bt_ps%d" % h)
            for t in range(PACK):
                nc.tensor.transpose(ps[:, P * t : P * (t + 1)], words[:, t : J : PACK], ident[:])
            b_in = sb.tile([P, 2 * P, PACK], BF16, name="b_in%d" % h, tag="b_in%d" % h, align_bytes=64)
            nc.scalar.copy(b_in[:], quarters(ps[:].bitcast(BF16)).rearrange("p t c -> p c t"))
            return b_in

        def product(name, bq, i_cols, where, tag):
            width = i_cols.stop - i_cols.start
            ps = bank(where, "gx_ps" + name)
            q, sc = bq
            for e in range(2):
                cols = slice(P * e, P * (e + 1))
                nc.tensor.matmul_mx(out=ps[:, width * e : width * (e + 1)], lhsT=q[:, cols].bitcast(FP8X4), lhsT_scale=sc[:, cols],
                                    rhs=gq[:, i_cols].bitcast(FP8X4), rhs_scale=gsc[:, i_cols], start=True, stop=True)
            gx = sb.tile([P, 2 * width], F32, name="gx" + name, tag=tag, align_bytes=64)
            nc.scalar.copy(gx[:], ps[:, 0 : 2 * width])
            return [gx[:, 0:width], gx[:, width : 2 * width]]

        def put(k, gx, i_cols):
            nc.vector.tensor_copy(gf[k][:].indirect(o1[:, i_cols.start // 16 : i_cols.stop // 16]), gx)

        def turn_faded(ps, k, u, closed):
            for c in range(4):
                nc.tensor.matmul(ps[:, P * c : P * (c + 1)], lhsT=faded[4 * u + c][:, P * k : P * (k + 1)], rhs=ident[:], is_transpose=True,
                                 start=(c == 0), stop=(closed and c == 3))

        def finish(k, u, where, pieces):
            ps = bank(where, "back%d_%d" % (k, u))
            turn_faded(ps, k, u, True)
            width = BANK // pieces
            for v in range(pieces):
                res = sb.tile([P, width], F32, name="res%d_%d_%d" % (k, u, v))
                cols = slice(BANK * u + width * v, BANK * u + width * (v + 1))
                nc.vector.tensor_tensor(res[:], ps[:, width * v : width * (v + 1)], gf[k][:, cols], ALU.add)
                nc.sync.dma_start(out[P * k : P * (k + 1), cols], res[:])

        def faded_rows(k, u, where):
            ps = bank(where, "back%d_%d" % (k, u))
            turn_faded(ps, k, u, True)
            t = sb.tile([P, BANK], F32, name="faded_rows%d_%d" % (k, u))
            nc.scalar.copy(t[:], ps[:])
            return t

        def finish_on_gpsimd(k, u, rows):
            res = sb.tile([P, BANK], F32, name="res%d_%d" % (k, u))
            cols = slice(BANK * u, BANK * (u + 1))
            nc.gpsimd.tensor_tensor(res[:], rows[:], gf[k][:, cols], ALU.add)
            nc.sync.dma_start(out[P * k : P * (k + 1), cols], res[:])

        faded = []

        def fade_block(c, where):
            ps = bank(where, "old_ps%d" % c)
            for k in range(4):
                nc.tensor.transpose(ps[:, P * k : P * (k + 1)], old_sb[c // 4][:, k, P * (c % 4) : P * (c % 4 + 1)], ident[:])
            f = sb.tile([P, D], F32, name="faded%d" % c)
            nc.scalar.activation(f[:], ps[:], ACT.Copy, scale=fade_col[:, c : c + 1])
            faded.append(f)

        first, second, both = slice(0, P), slice(P, I), slice(0, I)
        old_banks = (4, 5, 6, 7, 3, 1, 6, 5)
        pair = [sb.tile([P, U], F32, name="pair%d" % h, tag=("aq1", "pair1")[h], align_bytes=64) for h in range(2)]
        sigmoid(0)
        scores_out(0)
        sigmoid(1)
        square(0)
        cast_half(0, pair[0], 0)
        cast_half(0, pair[0], 1)
        scores_out(1)
        square(1)
        for c in range(4):
            fade_block(c, old_banks[c])
        cast_half(1, pair[1], 0)

        a0 = linked(0, "a_term0")
        s1_0 = placed(0, "s1_0")
        a1 = linked(1, "a_term1")
        b0 = slope_term(0, s1_0, "old0")
        gs0 = turn(0, a0, b0, 2)
        b_in0 = turn_words(0, gather_words(0, pair[0], "bw0"), 4)
        cast_half(1, pair[1], 1)
        s1_1 = placed(1, "s1_0")
        g_in0 = scale_round(0, gs0, "g1")
        b1 = slope_term(1, s1_1, "b_term1")
        gs1 = turn(1, a1, b1, 5)
        quantise_gradient(0, g_in0)
        bq0 = quantise("b0", b_in0, 2 * P)
        words1 = gather_words(1, pair[1], "bw1")
        quantise_gradient(1, scale_round(1, gs1, "b_raw1"))
        gx_first = product("a", bq0, first, 6, "njs")
        b_in1 = turn_words(1, words1, 4)
        gx_second = product("b", bq0, second, 2, "gxb")
        put(0, gx_first[0], first)
        put(1, gx_first[1], first)
        put(0, gx_second[0], second)
        put(1, gx_second[1], second)
        bq1 = quantise("b1", b_in1, 2 * P)
        gx_both = product("c", bq1, both, 4, "gxc")
        rows = [faded_rows(k, 0, (0, 7, 3, 1)[k]) for k in range(4)]
        for c in range(4, 8):
            fade_block(c, old_banks[c])
        finish_on_gpsimd(0, 0, rows[0])
        finish_on_gpsimd(1, 0, rows[1])
        put(2, gx_both[0], both)
        finish_on_gpsimd(2, 0, rows[2])
        put(3, gx_both[1], both)
        finish_on_gpsimd(3, 0, rows[3])
        for k in range(4):
            finish(k, 1, (0, 7, 2, 3)[k], 2 if k == 3 else 1)
